import numpy as np
import ml_dtypes


def mxq(x, axis, fmt="e4m3"):
    dtype, down = {"e4m3": (ml_dtypes.float8_e4m3fn, 7), "e5m2": (ml_dtypes.float8_e5m2, 14)}[fmt]
    v = np.moveaxis(np.asarray(x, np.float32).astype(ml_dtypes.bfloat16).astype(np.float64), axis, -1)
    blocks = v.reshape(v.shape[:-1] + (-1, 32))
    amax = np.abs(blocks).max(-1, keepdims=True)
    byte = np.maximum(np.where(amax > 0, np.frexp(amax)[1] - 1 + 127, 0) - down, 1)
    scale = np.exp2(byte - 127.0)
    codes = (blocks / scale).astype(np.float32).astype(dtype).astype(np.float64)
    return np.moveaxis((codes * scale).reshape(v.shape), -1, axis)


WIDE = False


def mx_kscale(k):
    if not WIDE:
        return np.ones(k)
    levels = np.array([10, -10, 5, -5, 0])
    if k % 512:
        return np.exp2(np.random.permutation(np.resize(levels, k // 32))).repeat(32)
    a = np.empty((k // 512, 16))
    for p in range(k // 512):
        a[p, :8] = np.random.permutation(np.resize(levels, 8))
        for g in range(8):
            far = levels[np.abs(levels - a[p, g]) >= 10]
            a[p, g + 8] = far[np.random.randint(len(far))]
    return np.exp2(a.ravel()).repeat(32)


def f64(x):
    return np.asarray(x).astype(np.float64)


def striped(idx):
    return np.tile(idx.reshape(-1, 16).T, (8, 1)).astype(np.uint16)


def unstriped(offs):
    return offs[:16].T.reshape(-1).astype(np.int64)


def pack_weight(w):
    k, n = w.shape
    w = f64(np.asarray(w, np.float32).astype(ml_dtypes.bfloat16)).reshape(k // 32, 32, n)
    amax = np.abs(w).max(1)
    byte = np.clip(np.where(amax > 0, np.frexp(amax)[1] - 1 + 127 - 7, 1), 1, 254)
    scaled = (w * np.exp2(127.0 - byte)[:, None, :]).reshape(k, n).astype(np.float32)
    words = np.ascontiguousarray(scaled.reshape(k // 512, 128, 4, n).transpose(0, 1, 3, 2)).astype(ml_dtypes.float8_e4m3fn).view(np.uint8)
    return words, np.ascontiguousarray(byte.astype(np.uint8).reshape(k // 512, 16, n))


def unpack_weight(words, scales):
    g, p, n, _ = words.shape
    vals = np.ascontiguousarray(words).view(ml_dtypes.float8_e4m3fn).astype(np.float64) * np.repeat(np.exp2(scales.astype(np.float64) - 127.0), 8, axis=1)[..., None]
    return vals.transpose(0, 1, 3, 2).reshape(g * 512, n)


K, T, S, D, N = 512, 2048, 512, 4, 256


def setup_inputs():
    n = np.random.standard_normal
    s = mx_kscale(K)[:, None]
    packed_xT = pack_weight(n((K, T)) * s)
    packed_eT = pack_weight(n((K, T)) * s)
    return {
        "x_words": packed_xT[0],
        "x_scales": packed_xT[1],
        "e_words": packed_eT[0],
        "e_scales": packed_eT[1],
        "wr": (n((K, N)) / np.sqrt(2 * K) / s).astype(np.float32),
        "wi": (n((K, N)) / np.sqrt(2 * K) / s).astype(np.float32),
        "yr": (n((N, S))).astype(np.float32),
        "yi": (n((N, S))).astype(np.float32),
        "offs": striped(np.random.permutation(T)[:S]),
    }


def reference(x_words, x_scales, e_words, e_scales, wr, wi, yr, yi, offs):
    xq = unpack_weight(x_words, x_scales)[:, unstriped(offs)]
    wrq = mxq(f64(wr), 0, "e4m3")
    e_offs = unpack_weight(e_words, e_scales)[:, unstriped(offs)]
    wiq = mxq(f64(wi), 0, "e4m3")
    t0 = wiq.T @ e_offs
    hr = (wrq.T @ xq) - t0
    hi = wrq.T @ e_offs + wiq.T @ xq
    h2 = (hr) ** 2 + (hi) ** 2
    nn = h2.reshape(len(h2), -1, D).sum(axis=2) + 0.2
    hy = hr * f64(yr) + hi * f64(yi)
    z = (hy.reshape(len(hy), -1, D).sum(axis=2)) / nn
    az = np.abs(z)
    return nn * (-1.0 * az + 0.6)

@@ -1,0 +1,179 @@
+import math
+from contextlib import ExitStack
+
+import concourse.mybir as mybir
+from concourse.masks import make_identity
+
+K, T, S, D, N = 512, 2048, 512, 4, 256
+FLOPS = 4 * 2 * K * N * S
+
+F32 = mybir.dt.float32
+BF16 = mybir.dt.bfloat16
+I32 = mybir.dt.int32
+U32 = mybir.dt.uint32
+U16 = mybir.dt.uint16
+U8 = mybir.dt.uint8
+FP8X4 = mybir.dt.float8_e4m3fn_x4
+ACT = mybir.ActivationFunctionType
+ALU = mybir.AluOpType
+
+P = 128
+PACK = 4
+BLOCKS = N // P
+HALVES = 2
+HALF = S // HALVES
+HV = HALF // D
+
+
+def tile_picked_yqam_second_p_kernel(
+    tc, x_words, x_scales, e_words, e_scales, wr, wi, yr, yi, offs, out
+):
+    nc = tc.nc
+    with ExitStack() as ctx:
+        keep = ctx.enter_context(tc.tile_pool(name="keep", bufs=1))
+        psum = ctx.enter_context(tc.psum_pool(name="psum", bufs=1))
+
+        offsets = keep.tile([P, S // 16], U16, name="offsets")
+        nc.sync.dma_start(offsets[:], offs)
+
+        windows = []
+        for name in ("x", "e"):
+            win = keep.tile([P, T], U8, name=name + "_scale_window", align_bytes=64)
+            nc.vector.memset(win[:].bitcast(I32), 0)
+            windows.append(win)
+        identity = keep.tile([P, P], F32, name="identity")
+        nc.vector.memset(identity[:], 0.0)
+        make_identity(nc, identity[:], nomemset=True)
+
+        wi_raw = keep.tile([P, PACK, N], F32, name="wi_raw")
+        nc.sync.dma_start(wi_raw[:], wi.rearrange("(p j) n -> p j n", j=PACK))
+        for win, table in zip(windows, (x_scales, e_scales)):
+            nc.scalar.dma_start(win[0:P:8, :].bitcast(I32), table[0].bitcast(I32))
+        x_window = keep.tile([P, T], I32, name="x_window", align_bytes=64)
+        nc.sync.dma_start(x_window[:], x_words[0].rearrange("p n t -> p (n t)").bitcast(I32))
+
+        wr_raw = keep.tile([P, PACK, N], F32, name="wr_raw")
+        nc.sync.dma_start(wr_raw[:], wr.rearrange("(p j) n -> p j n", j=PACK))
+
+        e_window = keep.tile([P, T], I32, name="e_window", align_bytes=64)
+        nc.sync.dma_start(e_window[:], e_words[0].rearrange("p n t -> p (n t)").bitcast(I32))
+
+        picked_bytes = keep.tile([P, 2 * S], U8, name="picked_bytes", align_bytes=64)
+        for i, win in enumerate(windows):
+            nc.vector.tensor_copy(picked_bytes[:, i * S : (i + 1) * S], win[:].indirect(offsets[:]))
+        planes = keep.tile([P, 2 * S], U8, name="planes", align_bytes=64)
+        nc.vector.tensor_copy(planes[:].bitcast(I32), picked_bytes[:].bitcast(I32))
+        for r in range(1, 4):
+            nc.scalar.dma_start(planes[r:P:32, :].bitcast(I32), picked_bytes[8 * r : P : 32, :].bitcast(I32))
+
+        y = {}
+        for b in range(BLOCKS):
+            y[b] = keep.tile([P, 2, S], F32, name=f"y_{b}")
+            for c, table in enumerate((yr, yi)):
+                nc.sync.dma_start(y[b][:, c, :], table[b * P : (b + 1) * P, :])
+
+        def grouped_view(t):
+            return t[:].rearrange("p (c i) j -> p c j i", i=4)
+
+        def raw_view(t):
+            return t[:].rearrange("p j (c i) -> p c j i", i=4)
+
+        neg_bf = keep.tile([P, N, PACK], BF16, name="neg_bf", align_bytes=64)
+        nc.scalar.activation(grouped_view(neg_bf), raw_view(wi_raw), ACT.Copy, scale=-1.0)
+        wi_bf = keep.tile([P, N, PACK], BF16, name="wi_bf", align_bytes=64)
+        nc.scalar.copy(grouped_view(wi_bf), raw_view(wi_raw))
+        wr_bf = keep.tile([P, N, PACK], BF16, name="wr_bf", align_bytes=64)
+        nc.scalar.copy(grouped_view(wr_bf), raw_view(wr_raw))
+
+        quant = {}
+        for name, src in (("neg", neg_bf), ("wi", wi_bf), ("wr", wr_bf)):
+            codes = keep.tile([P, N], U32, name=name + "_codes", align_bytes=64)
+            scales = keep.tile([P, N], U8, name=name + "_scales", align_bytes=64)
+            nc.vector.quantize_mx(out=codes[:].bitcast(FP8X4), scales=scales[:], in_=src[:].rearrange("p n j -> p (n j)"))
+            quant[name] = (codes, scales)
+
+        x_picked = keep.tile([P, S], U32, name="x_picked", align_bytes=64)
+        nc.vector.tensor_copy(x_picked[:], x_window[:].bitcast(U32).indirect(offsets[:]))
+        e_picked = []
+        for h in range(HALVES):
+            part = keep.tile([P, HALF], U32, name=f"e_picked_{h}", align_bytes=64)
+            cols = slice(h * HALF // 16, (h + 1) * HALF // 16)
+            nc.vector.tensor_copy(part[:], e_window[:].bitcast(U32).indirect(offsets[:, cols]))
+            e_picked.append(part)
+
+        def product(acc, weight, b, words, plane, start, stop):
+            codes, scales = quant[weight]
+            rows = slice(b * P, (b + 1) * P)
+            nc.tensor.matmul_mx(
+                out=acc, lhsT=codes[:, rows].bitcast(FP8X4), lhsT_scale=scales[:, rows],
+                rhs=words.bitcast(FP8X4), rhs_scale=plane, start=start, stop=stop,
+            )
+
+        chunks = [(b, h) for b in range(BLOCKS) for h in range(HALVES)]
+        acc = {(b, h): psum.tile([P, 2, HALF], F32, name=f"acc_{b}_{h}") for b, h in chunks}
+        for c, weight in ((1, "wi"), (0, "wr")):
+            for h, b in chunks:
+                product(acc[b, h][:, c, :], weight, b, x_picked[:, h * HALF : (h + 1) * HALF],
+                        planes[:, h * HALF : (h + 1) * HALF], c == 1, False)
+        for h, b in chunks:
+            for c, weight in enumerate(("neg", "wr")):
+                product(acc[b, h][:, c, :], weight, b, e_picked[h][:],
+                        planes[:, S + h * HALF : S + (h + 1) * HALF], False, c == 1)
+
+        sq = [keep.tile([P, 2, D, S // D], F32, name=f"sq_{b}") for b in range(BLOCKS)]
+        total = [keep.tile([P, S // D], F32, name=f"total_{b}") for b in range(BLOCKS)]
+        magnitude = [keep.tile([P, S // D], F32, name=f"magnitude_{b}") for b in range(BLOCKS)]
+        prod = {}
+        power = {}
+
+        def multiply(b, h):
+            prod[b, h] = keep.tile([P, 2, HALF], F32, name=f"prod_{b}_{h}")
+            nc.vector.tensor_tensor(prod[b, h][:], acc[b, h][:], y[b][:, :, h * HALF : (h + 1) * HALF], ALU.mult)
+
+        def square(b, h):
+            nc.scalar.activation(sq[b][:, :, :, h * HV : (h + 1) * HV], acc[b, h][:].rearrange("p c (v d) -> p c d v", d=D),
+                                 ACT.Square, scale=math.sqrt(0.6))
+
+        def combine(b, h):
+            vs = slice(h * HV, (h + 1) * HV)
+            if (b, h) in ():
+                both = keep.tile([P, HALF], F32, name=f"both_{b}_{h}")
+                nc.gpsimd.tensor_tensor(both[:], prod[b, h][:, 0, :], prod[b, h][:, 1, :], ALU.add)
+                nc.vector.tensor_reduce(total[b][:, vs], both[:].rearrange("p (v d) -> p v d", d=D), mybir.AxisListType.X, ALU.add)
+            else:
+                nc.vector.tensor_reduce(total[b][:, vs], prod[b, h][:].rearrange("p c (v d) -> p v c d", d=D), mybir.AxisListType.XY, ALU.add)
+            if (b, h) == (1, 1) and True:
+                nc.vector.scalar_tensor_tensor(magnitude[b][:, vs], total[b][:, vs], -1.0, total[b][:, vs], ALU.mult, ALU.max)
+            else:
+                nc.scalar.activation(magnitude[b][:, vs], total[b][:, vs], ACT.Abs)
+
+        def sum_squares(b):
+            turned = psum.tile([P, P], F32, name=f"turned_{b}")
+            for i in range(2 * D):
+                nc.tensor.matmul(turned[:], sq[b][:, i // D, i % D, :], identity[:], start=(i == 0), stop=(i == 2 * D - 1), is_transpose=True)
+            turned_sb = keep.tile([P, P], F32, name=f"turned_sb_{b}")
+            nc.scalar.copy(turned_sb[:], turned[:])
+            power[b] = psum.tile([P, P], F32, name=f"power_{b}")
+            nc.tensor.transpose(power[b][:], turned_sb[:], identity[:])
+
+        def finish(b):
+            result = keep.tile([P, S // D], F32, name=f"result_{b}")
+            nc.vector.scalar_tensor_tensor(result[:], power[b][:], 0.12, magnitude[b][:], ALU.add, ALU.subtract)
+            nc.sync.dma_start(out[b * P : (b + 1) * P, :], result[:])
+
+        square(1, 0)
+        square(1, 1)
+        multiply(0, 0)
+        multiply(0, 1)
+        square(0, 0)
+        square(0, 1)
+        sum_squares(1)
+        sum_squares(0)
+        combine(0, 0)
+        multiply(1, 0)
+        combine(0, 1)
+        multiply(1, 1)
+        combine(1, 0)
+        combine(1, 1)
+        finish(0)
+        finish(1)

@@ -39,32 +39,41 @@ def tile_picked_yqam_second_p_kernel(
         windows = []
         for name in ("x", "e"):
             win = keep.tile([P, T], U8, name=name + "_scale_window", align_bytes=64)
-            nc.vector.memset(win[:].bitcast(I32), 0)
+            (nc.vector if name == "x" else nc.gpsimd).memset(win[:].bitcast(I32), 0)
             windows.append(win)
+        planes = []
+        for name in ("x", "e"):
+            plane = keep.tile([P, S], U8, name=name + "_plane", align_bytes=64)
+            nc.vector.memset(plane[:].bitcast(I32), 0)
+            planes.append(plane)
         identity = keep.tile([P, P], F32, name="identity")
-        nc.vector.memset(identity[:], 0.0)
-        make_identity(nc, identity[:], nomemset=True)
+        make_identity(nc, identity[:])
 
+        wr_raw = keep.tile([P, PACK, N], F32, name="wr_raw")
+        wr_rows = wr.rearrange("(p j) n -> p j n", j=PACK)
+        nc.sync.dma_start(wr_raw[:, :3, :], wr_rows[:, :3, :])
+        nc.sync.dma_start(windows[0][0:P:8, :].bitcast(I32), x_scales[0].bitcast(I32))
         wi_raw = keep.tile([P, PACK, N], F32, name="wi_raw")
         nc.sync.dma_start(wi_raw[:], wi.rearrange("(p j) n -> p j n", j=PACK))
-        for win, table in zip(windows, (x_scales, e_scales)):
-            nc.scalar.dma_start(win[0:P:8, :].bitcast(I32), table[0].bitcast(I32))
+        nc.sync.dma_start(windows[1][0:P:8, :].bitcast(I32), e_scales[0].bitcast(I32))
         x_window = keep.tile([P, T], I32, name="x_window", align_bytes=64)
         nc.sync.dma_start(x_window[:], x_words[0].rearrange("p n t -> p (n t)").bitcast(I32))
 
-        wr_raw = keep.tile([P, PACK, N], F32, name="wr_raw")
-        nc.sync.dma_start(wr_raw[:], wr.rearrange("(p j) n -> p j n", j=PACK))
+        nc.sync.dma_start(wr_raw[:, 3:, :], wr_rows[:, 3:, :])
 
         e_window = keep.tile([P, T], I32, name="e_window", align_bytes=64)
-        nc.sync.dma_start(e_window[:], e_words[0].rearrange("p n t -> p (n t)").bitcast(I32))
+        e_rows = e_words[0].rearrange("p n t -> p (n t)").bitcast(I32)
 
-        picked_bytes = keep.tile([P, 2 * S], U8, name="picked_bytes", align_bytes=64)
-        for i, win in enumerate(windows):
-            nc.vector.tensor_copy(picked_bytes[:, i * S : (i + 1) * S], win[:].indirect(offsets[:]))
-        planes = keep.tile([P, 2 * S], U8, name="planes", align_bytes=64)
-        nc.vector.tensor_copy(planes[:].bitcast(I32), picked_bytes[:].bitcast(I32))
-        for r in range(1, 4):
-            nc.scalar.dma_start(planes[r:P:32, :].bitcast(I32), picked_bytes[8 * r : P : 32, :].bitcast(I32))
+        def pick_scales(name, win, plane):
+            picked = keep.tile([P, S], U8, name=name + "_picked_bytes", align_bytes=64)
+            nc.vector.tensor_copy(picked[:], win[:].indirect(offsets[:]))
+            for r in range(4):
+                nc.sync.dma_start(plane[r:P:32, :].bitcast(I32), picked[8 * r : P : 32, :].bitcast(I32))
+            return plane
+
+        x_plane = pick_scales("x", windows[0], planes[0])
+        nc.sync.dma_start(e_window[:], e_rows)
+        e_plane = pick_scales("e", windows[1], planes[1])
 
         y = {}
         for b in range(BLOCKS):
@@ -78,28 +87,36 @@ def tile_picked_yqam_second_p_kernel(
         def raw_view(t):
             return t[:].rearrange("p j (c i) -> p c j i", i=4)
 
+        wi_bf = keep.tile([P, N, PACK], BF16, name="wi_bf", align_bytes=64)
+        nc.scalar.activation(grouped_view(wi_bf), raw_view(wi_raw), ACT.Copy)
         neg_bf = keep.tile([P, N, PACK], BF16, name="neg_bf", align_bytes=64)
         nc.scalar.activation(grouped_view(neg_bf), raw_view(wi_raw), ACT.Copy, scale=-1.0)
-        wi_bf = keep.tile([P, N, PACK], BF16, name="wi_bf", align_bytes=64)
-        nc.scalar.copy(grouped_view(wi_bf), raw_view(wi_raw))
         wr_bf = keep.tile([P, N, PACK], BF16, name="wr_bf", align_bytes=64)
-        nc.scalar.copy(grouped_view(wr_bf), raw_view(wr_raw))
+        nc.scalar.copy(grouped_view(wr_bf)[:, P // 4 :], raw_view(wr_raw)[:, P // 4 :])
 
         quant = {}
-        for name, src in (("neg", neg_bf), ("wi", wi_bf), ("wr", wr_bf)):
+
+        def quantise(name, src):
             codes = keep.tile([P, N], U32, name=name + "_codes", align_bytes=64)
             scales = keep.tile([P, N], U8, name=name + "_scales", align_bytes=64)
             nc.vector.quantize_mx(out=codes[:].bitcast(FP8X4), scales=scales[:], in_=src[:].rearrange("p n j -> p (n j)"))
             quant[name] = (codes, scales)
 
-        x_picked = keep.tile([P, S], U32, name="x_picked", align_bytes=64)
-        nc.vector.tensor_copy(x_picked[:], x_window[:].bitcast(U32).indirect(offsets[:]))
-        e_picked = []
-        for h in range(HALVES):
-            part = keep.tile([P, HALF], U32, name=f"e_picked_{h}", align_bytes=64)
-            cols = slice(h * HALF // 16, (h + 1) * HALF // 16)
-            nc.vector.tensor_copy(part[:], e_window[:].bitcast(U32).indirect(offsets[:, cols]))
-            e_picked.append(part)
+        def pick_words(name, window):
+            parts = []
+            for h in range(HALVES):
+                part = keep.tile([P, HALF], U32, name=f"{name}_picked_{h}", align_bytes=64)
+                cols = slice(h * HALF // 16, (h + 1) * HALF // 16)
+                nc.vector.tensor_copy(part[:], window[:].bitcast(U32).indirect(offsets[:, cols]))
+                parts.append(part)
+            return parts
+
+        quantise("wi", wi_bf)
+        x_picked = pick_words("x", x_window)
+        nc.vector.tensor_copy(grouped_view(wr_bf)[:, : P // 4], raw_view(wr_raw)[:, : P // 4])
+        quantise("neg", neg_bf)
+        quantise("wr", wr_bf)
+        e_picked = pick_words("e", e_window)
 
         def product(acc, weight, b, words, plane, start, stop):
             codes, scales = quant[weight]
@@ -109,22 +126,25 @@ def tile_picked_yqam_second_p_kernel(
                 rhs=words.bitcast(FP8X4), rhs_scale=plane, start=start, stop=stop,
             )
 
+        warm = psum.tile([P, N], F32, name="warm", tag="turned_0")
+        for i in range(4):
+            product(warm[:], "wi", i % BLOCKS, quant["wi"][0][:], quant["wi"][1][:], True, True)
+
         chunks = [(b, h) for b in range(BLOCKS) for h in range(HALVES)]
         acc = {(b, h): psum.tile([P, 2, HALF], F32, name=f"acc_{b}_{h}") for b, h in chunks}
         for c, weight in ((1, "wi"), (0, "wr")):
             for h, b in chunks:
-                product(acc[b, h][:, c, :], weight, b, x_picked[:, h * HALF : (h + 1) * HALF],
-                        planes[:, h * HALF : (h + 1) * HALF], c == 1, False)
+                product(acc[b, h][:, c, :], weight, b, x_picked[h][:],
+                        x_plane[:, h * HALF : (h + 1) * HALF], c == 1, False)
         for h, b in chunks:
             for c, weight in enumerate(("neg", "wr")):
                 product(acc[b, h][:, c, :], weight, b, e_picked[h][:],
-                        planes[:, S + h * HALF : S + (h + 1) * HALF], False, c == 1)
+                        e_plane[:, h * HALF : (h + 1) * HALF], False, c == 1)
 
         sq = [keep.tile([P, 2, D, S // D], F32, name=f"sq_{b}") for b in range(BLOCKS)]
         total = [keep.tile([P, S // D], F32, name=f"total_{b}") for b in range(BLOCKS)]
         magnitude = [keep.tile([P, S // D], F32, name=f"magnitude_{b}") for b in range(BLOCKS)]
         prod = {}
-        power = {}
 
         def multiply(b, h):
             prod[b, h] = keep.tile([P, 2, HALF], F32, name=f"prod_{b}_{h}")
@@ -136,27 +156,30 @@ def tile_picked_yqam_second_p_kernel(
 
         def combine(b, h):
             vs = slice(h * HV, (h + 1) * HV)
-            if (b, h) in ():
+            if (b, h) in ((0, 0), (0, 1), (1, 0)):
                 both = keep.tile([P, HALF], F32, name=f"both_{b}_{h}")
                 nc.gpsimd.tensor_tensor(both[:], prod[b, h][:, 0, :], prod[b, h][:, 1, :], ALU.add)
                 nc.vector.tensor_reduce(total[b][:, vs], both[:].rearrange("p (v d) -> p v d", d=D), mybir.AxisListType.X, ALU.add)
             else:
                 nc.vector.tensor_reduce(total[b][:, vs], prod[b, h][:].rearrange("p c (v d) -> p v c d", d=D), mybir.AxisListType.XY, ALU.add)
-            if (b, h) == (1, 1) and True:
-                nc.vector.scalar_tensor_tensor(magnitude[b][:, vs], total[b][:, vs], -1.0, total[b][:, vs], ALU.mult, ALU.max)
-            else:
-                nc.scalar.activation(magnitude[b][:, vs], total[b][:, vs], ACT.Abs)
+
+        turned = [psum.tile([P, P], F32, name=f"turned_{b}", tag=f"turned_{b}") for b in range(BLOCKS)]
+        power = [psum.tile([P, P], F32, name=f"power_{b}") for b in range(BLOCKS)]
 
         def sum_squares(b):
-            turned = psum.tile([P, P], F32, name=f"turned_{b}")
             for i in range(2 * D):
-                nc.tensor.matmul(turned[:], sq[b][:, i // D, i % D, :], identity[:], start=(i == 0), stop=(i == 2 * D - 1), is_transpose=True)
+                nc.tensor.matmul(turned[b][:], sq[b][:, i // D, i % D, :], identity[:], start=(i == 0), stop=(i == 2 * D - 1), is_transpose=True)
+
+        def turn_back(b):
             turned_sb = keep.tile([P, P], F32, name=f"turned_sb_{b}")
-            nc.scalar.copy(turned_sb[:], turned[:])
-            power[b] = psum.tile([P, P], F32, name=f"power_{b}")
+            nc.scalar.copy(turned_sb[:], turned[b][:])
             nc.tensor.transpose(power[b][:], turned_sb[:], identity[:])
 
         def finish(b):
+            if b == 1:
+                nc.vector.scalar_tensor_tensor(magnitude[b][:], total[b][:], -1.0, total[b][:], ALU.mult, ALU.max)
+            else:
+                nc.scalar.activation(magnitude[b][:], total[b][:], ACT.Abs)
             result = keep.tile([P, S // D], F32, name=f"result_{b}")
             nc.vector.scalar_tensor_tensor(result[:], power[b][:], 0.12, magnitude[b][:], ALU.add, ALU.subtract)
             nc.sync.dma_start(out[b * P : (b + 1) * P, :], result[:])
@@ -169,11 +192,13 @@ def tile_picked_yqam_second_p_kernel(
         square(0, 1)
         sum_squares(1)
         sum_squares(0)
-        combine(0, 0)
+        turn_back(1)
+        turn_back(0)
         multiply(1, 0)
-        combine(0, 1)
         multiply(1, 1)
-        combine(1, 0)
+        combine(0, 0)
         combine(1, 1)
-        finish(0)
+        combine(0, 1)
+        combine(1, 0)
         finish(1)
+        finish(0)

@@ -23,6 +23,8 @@ BLOCKS = N // P
 HALVES = 2
 HALF = S // HALVES
 HV = HALF // D
+SCALE_AT = P - 16
+E_HEAD = 512
 
 
 def tile_picked_yqam_second_p_kernel(
@@ -37,43 +39,34 @@ def tile_picked_yqam_second_p_kernel(
         nc.sync.dma_start(offsets[:], offs)
 
         windows = []
-        for name in ("x", "e"):
+        for name, table in (("x", x_scales), ("e", e_scales)):
             win = keep.tile([P, T], U8, name=name + "_scale_window", align_bytes=64)
-            (nc.vector if name == "x" else nc.gpsimd).memset(win[:].bitcast(I32), 0)
+            (nc.vector if name == "x" else nc.gpsimd).memset(win[:SCALE_AT, :].bitcast(I32), 0)
+            nc.sync.dma_start(win[SCALE_AT:, :].bitcast(I32), table[0].bitcast(I32))
             windows.append(win)
-        planes = []
-        for name in ("x", "e"):
-            plane = keep.tile([P, S], U8, name=name + "_plane", align_bytes=64)
-            nc.vector.memset(plane[:].bitcast(I32), 0)
-            planes.append(plane)
+        planes = keep.tile([P, 2 * S], U8, name="planes", align_bytes=64)
+        nc.vector.memset(planes[:].bitcast(I32), 0)
         identity = keep.tile([P, P], F32, name="identity")
         make_identity(nc, identity[:])
 
-        wr_raw = keep.tile([P, PACK, N], F32, name="wr_raw")
-        wr_rows = wr.rearrange("(p j) n -> p j n", j=PACK)
-        nc.sync.dma_start(wr_raw[:, :3, :], wr_rows[:, :3, :])
-        nc.sync.dma_start(windows[0][0:P:8, :].bitcast(I32), x_scales[0].bitcast(I32))
         wi_raw = keep.tile([P, PACK, N], F32, name="wi_raw")
         nc.sync.dma_start(wi_raw[:], wi.rearrange("(p j) n -> p j n", j=PACK))
-        nc.sync.dma_start(windows[1][0:P:8, :].bitcast(I32), e_scales[0].bitcast(I32))
+        wr_raw = keep.tile([P, PACK, N], F32, name="wr_raw")
+        nc.sync.dma_start(wr_raw[:], wr.rearrange("(p j) n -> p j n", j=PACK))
         x_window = keep.tile([P, T], I32, name="x_window", align_bytes=64)
         nc.sync.dma_start(x_window[:], x_words[0].rearrange("p n t -> p (n t)").bitcast(I32))
-
-        nc.sync.dma_start(wr_raw[:, 3:, :], wr_rows[:, 3:, :])
-
         e_window = keep.tile([P, T], I32, name="e_window", align_bytes=64)
         e_rows = e_words[0].rearrange("p n t -> p (n t)").bitcast(I32)
+        nc.sync.dma_start(e_window[:, :E_HEAD], e_rows[:, :E_HEAD])
 
-        def pick_scales(name, win, plane):
-            picked = keep.tile([P, S], U8, name=name + "_picked_bytes", align_bytes=64)
-            nc.vector.tensor_copy(picked[:], win[:].indirect(offsets[:]))
-            for r in range(4):
-                nc.sync.dma_start(plane[r:P:32, :].bitcast(I32), picked[8 * r : P : 32, :].bitcast(I32))
-            return plane
+        picked_bytes = keep.tile([P, 2 * S], U8, name="picked_bytes", align_bytes=64)
+        for i, win in enumerate(windows):
+            nc.vector.tensor_copy(picked_bytes[:, i * S : (i + 1) * S], win[:].indirect(offsets[:]))
+        for q in range(4):
+            rows = slice(SCALE_AT + 4 * q, SCALE_AT + 4 * q + 4)
+            nc.sync.dma_start(planes[32 * q : 32 * q + 4, :].bitcast(I32), picked_bytes[rows, :].bitcast(I32))
 
-        x_plane = pick_scales("x", windows[0], planes[0])
-        nc.sync.dma_start(e_window[:], e_rows)
-        e_plane = pick_scales("e", windows[1], planes[1])
+        nc.sync.dma_start(e_window[:, E_HEAD:], e_rows[:, E_HEAD:])
 
         y = {}
         for b in range(BLOCKS):
@@ -88,11 +81,10 @@ def tile_picked_yqam_second_p_kernel(
             return t[:].rearrange("p j (c i) -> p c j i", i=4)
 
         wi_bf = keep.tile([P, N, PACK], BF16, name="wi_bf", align_bytes=64)
-        nc.scalar.activation(grouped_view(wi_bf), raw_view(wi_raw), ACT.Copy)
-        neg_bf = keep.tile([P, N, PACK], BF16, name="neg_bf", align_bytes=64)
-        nc.scalar.activation(grouped_view(neg_bf), raw_view(wi_raw), ACT.Copy, scale=-1.0)
+        nc.scalar.copy(grouped_view(wi_bf), raw_view(wi_raw))
         wr_bf = keep.tile([P, N, PACK], BF16, name="wr_bf", align_bytes=64)
         nc.scalar.copy(grouped_view(wr_bf)[:, P // 4 :], raw_view(wr_raw)[:, P // 4 :])
+        neg_bf = keep.tile([P, N, PACK], BF16, name="neg_bf", align_bytes=64)
 
         quant = {}
 
@@ -111,11 +103,12 @@ def tile_picked_yqam_second_p_kernel(
                 parts.append(part)
             return parts
 
+        nc.vector.tensor_scalar(neg_bf[:], wi_bf[:], -1.0, None, ALU.mult)
         quantise("wi", wi_bf)
-        x_picked = pick_words("x", x_window)
         nc.vector.tensor_copy(grouped_view(wr_bf)[:, : P // 4], raw_view(wr_raw)[:, : P // 4])
         quantise("neg", neg_bf)
         quantise("wr", wr_bf)
+        x_picked = pick_words("x", x_window)
         e_picked = pick_words("e", e_window)
 
         def product(acc, weight, b, words, plane, start, stop):
@@ -128,18 +121,18 @@ def tile_picked_yqam_second_p_kernel(
 
         warm = psum.tile([P, N], F32, name="warm", tag="turned_0")
         for i in range(4):
-            product(warm[:], "wi", i % BLOCKS, quant["wi"][0][:], quant["wi"][1][:], True, True)
+            product(warm[:], "neg", i % BLOCKS, quant["neg"][0][:], quant["neg"][1][:], True, True)
 
         chunks = [(b, h) for b in range(BLOCKS) for h in range(HALVES)]
         acc = {(b, h): psum.tile([P, 2, HALF], F32, name=f"acc_{b}_{h}") for b, h in chunks}
-        for c, weight in ((1, "wi"), (0, "wr")):
-            for h, b in chunks:
+        for h, b in chunks:
+            for c, weight in ((1, "wi"), (0, "wr")):
                 product(acc[b, h][:, c, :], weight, b, x_picked[h][:],
-                        x_plane[:, h * HALF : (h + 1) * HALF], c == 1, False)
+                        planes[:, h * HALF : (h + 1) * HALF], c == 1, False)
         for h, b in chunks:
             for c, weight in enumerate(("neg", "wr")):
                 product(acc[b, h][:, c, :], weight, b, e_picked[h][:],
-                        e_plane[:, h * HALF : (h + 1) * HALF], False, c == 1)
+                        planes[:, S + h * HALF : S + (h + 1) * HALF], False, c == 1)
 
         sq = [keep.tile([P, 2, D, S // D], F32, name=f"sq_{b}") for b in range(BLOCKS)]
         total = [keep.tile([P, S // D], F32, name=f"total_{b}") for b in range(BLOCKS)]

@@ -119,10 +119,6 @@ def tile_picked_yqam_second_p_kernel(
                 rhs=words.bitcast(FP8X4), rhs_scale=plane, start=start, stop=stop,
             )
 
-        warm = psum.tile([P, N], F32, name="warm", tag="turned_0")
-        for i in range(4):
-            product(warm[:], "neg", i % BLOCKS, quant["neg"][0][:], quant["neg"][1][:], True, True)
-
         chunks = [(b, h) for b in range(BLOCKS) for h in range(HALVES)]
         acc = {(b, h): psum.tile([P, 2, HALF], F32, name=f"acc_{b}_{h}") for b, h in chunks}
         for h, b in chunks:
@@ -144,8 +140,9 @@ def tile_picked_yqam_second_p_kernel(
             nc.vector.tensor_tensor(prod[b, h][:], acc[b, h][:], y[b][:, :, h * HALF : (h + 1) * HALF], ALU.mult)
 
         def square(b, h):
-            nc.scalar.activation(sq[b][:, :, :, h * HV : (h + 1) * HV], acc[b, h][:].rearrange("p c (v d) -> p c d v", d=D),
-                                 ACT.Square, scale=math.sqrt(0.6))
+            for cs in (slice(0, 1), slice(1, 2)) if (b, h) == (0, 1) else (slice(0, 2),):
+                nc.scalar.activation(sq[b][:, cs, :, h * HV : (h + 1) * HV], acc[b, h][:, cs, :].rearrange("p c (v d) -> p c d v", d=D),
+                                     ACT.Square, scale=math.sqrt(0.6))
 
         def combine(b, h):
             vs = slice(h * HV, (h + 1) * HV)
@@ -156,7 +153,7 @@ def tile_picked_yqam_second_p_kernel(
             else:
                 nc.vector.tensor_reduce(total[b][:, vs], prod[b, h][:].rearrange("p c (v d) -> p v c d", d=D), mybir.AxisListType.XY, ALU.add)
 
-        turned = [psum.tile([P, P], F32, name=f"turned_{b}", tag=f"turned_{b}") for b in range(BLOCKS)]
+        turned = [psum.tile([P, P], F32, name=f"turned_{b}") for b in range(BLOCKS)]
         power = [psum.tile([P, P], F32, name=f"power_{b}") for b in range(BLOCKS)]
 
         def sum_squares(b):

@@ -16,14 +16,19 @@ U8 = mybir.dt.uint8
 FP8X4 = mybir.dt.float8_e4m3fn_x4
 ACT = mybir.ActivationFunctionType
 ALU = mybir.AluOpType
+AXIS = mybir.AxisListType
 
 P = 128
 PACK = 4
+LINE = 4
 BLOCKS = N // P
 HALVES = 2
 HALF = S // HALVES
-HV = HALF // D
-SCALE_AT = P - 16
+GROUPS = S // D
+HALF_GROUPS = HALF // D
+RE, IM = 0, 1
+SCALE_ROWS = K // 32
+SCALE_AT = P - SCALE_ROWS
 E_HEAD = 512
 
 
@@ -39,9 +44,9 @@ def tile_picked_yqam_second_p_kernel(
         nc.sync.dma_start(offsets[:], offs)
 
         windows = []
-        for name, table in (("x", x_scales), ("e", e_scales)):
+        for name, table, clearer in (("x", x_scales, nc.vector), ("e", e_scales, nc.gpsimd)):
             win = keep.tile([P, T], U8, name=name + "_scale_window", align_bytes=64)
-            (nc.vector if name == "x" else nc.gpsimd).memset(win[:SCALE_AT, :].bitcast(I32), 0)
+            clearer.memset(win[:SCALE_AT, :].bitcast(I32), 0)
             nc.sync.dma_start(win[SCALE_AT:, :].bitcast(I32), table[0].bitcast(I32))
             windows.append(win)
         planes = keep.tile([P, 2 * S], U8, name="planes", align_bytes=64)
@@ -62,7 +67,7 @@ def tile_picked_yqam_second_p_kernel(
         picked_bytes = keep.tile([P, 2 * S], U8, name="picked_bytes", align_bytes=64)
         for i, win in enumerate(windows):
             nc.vector.tensor_copy(picked_bytes[:, i * S : (i + 1) * S], win[:].indirect(offsets[:]))
-        for q in range(4):
+        for q in range(SCALE_ROWS // 4):
             rows = slice(SCALE_AT + 4 * q, SCALE_AT + 4 * q + 4)
             nc.sync.dma_start(planes[32 * q : 32 * q + 4, :].bitcast(I32), picked_bytes[rows, :].bitcast(I32))
 
@@ -71,19 +76,20 @@ def tile_picked_yqam_second_p_kernel(
         y = {}
         for b in range(BLOCKS):
             y[b] = keep.tile([P, 2, S], F32, name=f"y_{b}")
-            for c, table in enumerate((yr, yi)):
-                nc.sync.dma_start(y[b][:, c, :], table[b * P : (b + 1) * P, :])
+            for part, table in ((RE, yr), (IM, yi)):
+                nc.sync.dma_start(y[b][:, part, :], table[b * P : (b + 1) * P, :])
 
-        def grouped_view(t):
-            return t[:].rearrange("p (c i) j -> p c j i", i=4)
+        def grouped_view(tile):
+            return tile[:].rearrange("p (c i) j -> p c j i", i=LINE)
 
-        def raw_view(t):
-            return t[:].rearrange("p j (c i) -> p c j i", i=4)
+        def raw_view(tile):
+            return tile[:].rearrange("p j (c i) -> p c j i", i=LINE)
 
+        first_block, second_block = slice(0, P // LINE), slice(P // LINE, N // LINE)
         wi_bf = keep.tile([P, N, PACK], BF16, name="wi_bf", align_bytes=64)
         nc.scalar.copy(grouped_view(wi_bf), raw_view(wi_raw))
         wr_bf = keep.tile([P, N, PACK], BF16, name="wr_bf", align_bytes=64)
-        nc.scalar.copy(grouped_view(wr_bf)[:, P // 4 :], raw_view(wr_raw)[:, P // 4 :])
+        nc.scalar.copy(grouped_view(wr_bf)[:, second_block], raw_view(wr_raw)[:, second_block])
         neg_bf = keep.tile([P, N, PACK], BF16, name="neg_bf", align_bytes=64)
 
         quant = {}
@@ -91,74 +97,87 @@ def tile_picked_yqam_second_p_kernel(
         def quantise(name, src):
             codes = keep.tile([P, N], U32, name=name + "_codes", align_bytes=64)
             scales = keep.tile([P, N], U8, name=name + "_scales", align_bytes=64)
-            nc.vector.quantize_mx(out=codes[:].bitcast(FP8X4), scales=scales[:], in_=src[:].rearrange("p n j -> p (n j)"))
+            nc.vector.quantize_mx(
+                out=codes[:].bitcast(FP8X4), scales=scales[:], in_=src[:].rearrange("p n j -> p (n j)")
+            )
             quant[name] = (codes, scales)
 
         def pick_words(name, window):
-            parts = []
+            halves = []
             for h in range(HALVES):
-                part = keep.tile([P, HALF], U32, name=f"{name}_picked_{h}", align_bytes=64)
+                picked = keep.tile([P, HALF], U32, name=f"{name}_picked_{h}", align_bytes=64)
                 cols = slice(h * HALF // 16, (h + 1) * HALF // 16)
-                nc.vector.tensor_copy(part[:], window[:].bitcast(U32).indirect(offsets[:, cols]))
-                parts.append(part)
-            return parts
+                nc.vector.tensor_copy(picked[:], window[:].bitcast(U32).indirect(offsets[:, cols]))
+                halves.append(picked)
+            return halves
 
         nc.vector.tensor_scalar(neg_bf[:], wi_bf[:], -1.0, None, ALU.mult)
         quantise("wi", wi_bf)
-        nc.vector.tensor_copy(grouped_view(wr_bf)[:, : P // 4], raw_view(wr_raw)[:, : P // 4])
+        nc.vector.tensor_copy(grouped_view(wr_bf)[:, first_block], raw_view(wr_raw)[:, first_block])
         quantise("neg", neg_bf)
         quantise("wr", wr_bf)
         x_picked = pick_words("x", x_window)
         e_picked = pick_words("e", e_window)
 
-        def product(acc, weight, b, words, plane, start, stop):
+        def entries(h, base=0):
+            return slice(base + h * HALF, base + (h + 1) * HALF)
+
+        def groups(h):
+            return slice(h * HALF_GROUPS, (h + 1) * HALF_GROUPS)
+
+        def product(dst, weight, b, words, plane, start, stop):
             codes, scales = quant[weight]
-            rows = slice(b * P, (b + 1) * P)
+            cols = slice(b * P, (b + 1) * P)
             nc.tensor.matmul_mx(
-                out=acc, lhsT=codes[:, rows].bitcast(FP8X4), lhsT_scale=scales[:, rows],
+                out=dst, lhsT=codes[:, cols].bitcast(FP8X4), lhsT_scale=scales[:, cols],
                 rhs=words.bitcast(FP8X4), rhs_scale=plane, start=start, stop=stop,
             )
 
-        chunks = [(b, h) for b in range(BLOCKS) for h in range(HALVES)]
-        acc = {(b, h): psum.tile([P, 2, HALF], F32, name=f"acc_{b}_{h}") for b, h in chunks}
-        for h, b in chunks:
-            for c, weight in ((1, "wi"), (0, "wr")):
-                product(acc[b, h][:, c, :], weight, b, x_picked[h][:],
-                        planes[:, h * HALF : (h + 1) * HALF], c == 1, False)
-        for h, b in chunks:
-            for c, weight in enumerate(("neg", "wr")):
-                product(acc[b, h][:, c, :], weight, b, e_picked[h][:],
-                        planes[:, S + h * HALF : S + (h + 1) * HALF], False, c == 1)
+        acc = {
+            (b, h): psum.tile([P, 2, HALF], F32, name=f"acc_{b}_{h}") for b in range(BLOCKS) for h in range(HALVES)
+        }
+        for h in range(HALVES):
+            for b in range(BLOCKS):
+                product(acc[b, h][:, IM, :], "wi", b, x_picked[h][:], planes[:, entries(h)], True, False)
+                product(acc[b, h][:, RE, :], "wr", b, x_picked[h][:], planes[:, entries(h)], False, False)
+        for h in range(HALVES):
+            for b in range(BLOCKS):
+                product(acc[b, h][:, RE, :], "neg", b, e_picked[h][:], planes[:, entries(h, S)], False, False)
+                product(acc[b, h][:, IM, :], "wr", b, e_picked[h][:], planes[:, entries(h, S)], False, True)
 
-        sq = [keep.tile([P, 2, D, S // D], F32, name=f"sq_{b}") for b in range(BLOCKS)]
-        total = [keep.tile([P, S // D], F32, name=f"total_{b}") for b in range(BLOCKS)]
-        magnitude = [keep.tile([P, S // D], F32, name=f"magnitude_{b}") for b in range(BLOCKS)]
-        prod = {}
+        sq = [keep.tile([P, 2, D, GROUPS], F32, name=f"sq_{b}") for b in range(BLOCKS)]
+        total = [keep.tile([P, GROUPS], F32, name=f"total_{b}") for b in range(BLOCKS)]
+        magnitude = [keep.tile([P, GROUPS], F32, name=f"magnitude_{b}") for b in range(BLOCKS)]
+        prod = [keep.tile([P, HALVES, 2, HALF], F32, name=f"prod_{b}") for b in range(BLOCKS)]
 
         def multiply(b, h):
-            prod[b, h] = keep.tile([P, 2, HALF], F32, name=f"prod_{b}_{h}")
-            nc.vector.tensor_tensor(prod[b, h][:], acc[b, h][:], y[b][:, :, h * HALF : (h + 1) * HALF], ALU.mult)
+            nc.vector.tensor_tensor(prod[b][:, h], acc[b, h][:], y[b][:, :, entries(h)], ALU.mult)
 
-        def square(b, h):
-            for cs in (slice(0, 1), slice(1, 2)) if (b, h) == (0, 1) else (slice(0, 2),):
-                nc.scalar.activation(sq[b][:, cs, :, h * HV : (h + 1) * HV], acc[b, h][:, cs, :].rearrange("p c (v d) -> p c d v", d=D),
-                                     ACT.Square, scale=math.sqrt(0.6))
+        def square(b, h, parts=slice(RE, IM + 1)):
+            nc.scalar.activation(
+                sq[b][:, parts, :, groups(h)], acc[b, h][:, parts, :].rearrange("p c (v d) -> p c d v", d=D),
+                ACT.Square, scale=math.sqrt(0.6),
+            )
 
-        def combine(b, h):
-            vs = slice(h * HV, (h + 1) * HV)
-            if (b, h) in ((0, 0), (0, 1), (1, 0)):
-                both = keep.tile([P, HALF], F32, name=f"both_{b}_{h}")
-                nc.gpsimd.tensor_tensor(both[:], prod[b, h][:, 0, :], prod[b, h][:, 1, :], ALU.add)
-                nc.vector.tensor_reduce(total[b][:, vs], both[:].rearrange("p (v d) -> p v d", d=D), mybir.AxisListType.X, ALU.add)
-            else:
-                nc.vector.tensor_reduce(total[b][:, vs], prod[b, h][:].rearrange("p c (v d) -> p v c d", d=D), mybir.AxisListType.XY, ALU.add)
+        def sum_products(b, h):
+            nc.vector.tensor_reduce(
+                total[b][:, groups(h)], prod[b][:, h].rearrange("p c (v d) -> p v c d", d=D), AXIS.XY, ALU.add
+            )
+
+        def sum_products_shared(b):
+            both = keep.tile([P, HALVES, HALF], F32, name=f"both_{b}")
+            nc.gpsimd.tensor_tensor(both[:], prod[b][:, :, RE, :], prod[b][:, :, IM, :], ALU.add)
+            nc.vector.tensor_reduce(total[b][:], both[:].rearrange("p h (v d) -> p (h v) d", d=D), AXIS.X, ALU.add)
 
         turned = [psum.tile([P, P], F32, name=f"turned_{b}") for b in range(BLOCKS)]
         power = [psum.tile([P, P], F32, name=f"power_{b}") for b in range(BLOCKS)]
 
         def sum_squares(b):
             for i in range(2 * D):
-                nc.tensor.matmul(turned[b][:], sq[b][:, i // D, i % D, :], identity[:], start=(i == 0), stop=(i == 2 * D - 1), is_transpose=True)
+                nc.tensor.matmul(
+                    turned[b][:], sq[b][:, i // D, i % D, :], identity[:],
+                    start=(i == 0), stop=(i == 2 * D - 1), is_transpose=True,
+                )
 
         def turn_back(b):
             turned_sb = keep.tile([P, P], F32, name=f"turned_sb_{b}")
@@ -166,11 +185,7 @@ def tile_picked_yqam_second_p_kernel(
             nc.tensor.transpose(power[b][:], turned_sb[:], identity[:])
 
         def finish(b):
-            if b == 1:
-                nc.vector.scalar_tensor_tensor(magnitude[b][:], total[b][:], -1.0, total[b][:], ALU.mult, ALU.max)
-            else:
-                nc.scalar.activation(magnitude[b][:], total[b][:], ACT.Abs)
-            result = keep.tile([P, S // D], F32, name=f"result_{b}")
+            result = keep.tile([P, GROUPS], F32, name=f"result_{b}")
             nc.vector.scalar_tensor_tensor(result[:], power[b][:], 0.12, magnitude[b][:], ALU.add, ALU.subtract)
             nc.sync.dma_start(out[b * P : (b + 1) * P, :], result[:])
 
@@ -179,16 +194,18 @@ def tile_picked_yqam_second_p_kernel(
         multiply(0, 0)
         multiply(0, 1)
         square(0, 0)
-        square(0, 1)
+        square(0, 1, slice(RE, RE + 1))
+        square(0, 1, slice(IM, IM + 1))
         sum_squares(1)
         sum_squares(0)
         turn_back(1)
         turn_back(0)
         multiply(1, 0)
         multiply(1, 1)
-        combine(0, 0)
-        combine(1, 1)
-        combine(0, 1)
-        combine(1, 0)
+        sum_products(1, 0)
+        sum_products_shared(0)
+        sum_products(1, 1)
+        nc.vector.scalar_tensor_tensor(magnitude[1][:], total[1][:], -1.0, total[1][:], ALU.mult, ALU.max)
         finish(1)
+        nc.scalar.activation(magnitude[0][:], total[0][:], ACT.Abs)
         finish(0)

import math
from contextlib import ExitStack

import concourse.mybir as mybir
from concourse.masks import make_identity

K, T, S, D, N = 512, 2048, 512, 4, 256
FLOPS = 4 * 2 * K * N * S

F32 = mybir.dt.float32
BF16 = mybir.dt.bfloat16
I32 = mybir.dt.int32
U32 = mybir.dt.uint32
U16 = mybir.dt.uint16
U8 = mybir.dt.uint8
FP8X4 = mybir.dt.float8_e4m3fn_x4
ACT = mybir.ActivationFunctionType
ALU = mybir.AluOpType
AXIS = mybir.AxisListType

P = 128
PACK = 4
LINE = 4
BLOCKS = N // P
HALVES = 2
HALF = S // HALVES
GROUPS = S // D
HALF_GROUPS = HALF // D
RE, IM = 0, 1
SCALE_ROWS = K // 32
SCALE_AT = P - SCALE_ROWS
E_HEAD = 512


def tile_picked_yqam_second_p_kernel(
    tc, x_words, x_scales, e_words, e_scales, wr, wi, yr, yi, offs, out
):
    nc = tc.nc
    with ExitStack() as ctx:
        keep = ctx.enter_context(tc.tile_pool(name="keep", bufs=1))
        psum = ctx.enter_context(tc.psum_pool(name="psum", bufs=1))

        offsets = keep.tile([P, S // 16], U16, name="offsets")
        nc.sync.dma_start(offsets[:], offs)

        windows = []
        for name, table, clearer in (("x", x_scales, nc.vector), ("e", e_scales, nc.gpsimd)):
            win = keep.tile([P, T], U8, name=name + "_scale_window", align_bytes=64)
            clearer.memset(win[:SCALE_AT, :].bitcast(I32), 0)
            nc.sync.dma_start(win[SCALE_AT:, :].bitcast(I32), table[0].bitcast(I32))
            windows.append(win)
        planes = keep.tile([P, 2 * S], U8, name="planes", align_bytes=64)
        nc.vector.memset(planes[:].bitcast(I32), 0)
        identity = keep.tile([P, P], F32, name="identity")
        make_identity(nc, identity[:])

        wi_raw = keep.tile([P, PACK, N], F32, name="wi_raw")
        nc.sync.dma_start(wi_raw[:], wi.rearrange("(p j) n -> p j n", j=PACK))
        wr_raw = keep.tile([P, PACK, N], F32, name="wr_raw")
        nc.sync.dma_start(wr_raw[:], wr.rearrange("(p j) n -> p j n", j=PACK))
        x_window = keep.tile([P, T], I32, name="x_window", align_bytes=64)
        nc.sync.dma_start(x_window[:], x_words[0].rearrange("p n t -> p (n t)").bitcast(I32))
        e_window = keep.tile([P, T], I32, name="e_window", align_bytes=64)
        e_rows = e_words[0].rearrange("p n t -> p (n t)").bitcast(I32)
        nc.sync.dma_start(e_window[:, :E_HEAD], e_rows[:, :E_HEAD])

        picked_bytes = keep.tile([P, 2 * S], U8, name="picked_bytes", align_bytes=64)
        for i, win in enumerate(windows):
            nc.vector.tensor_copy(picked_bytes[:, i * S : (i + 1) * S], win[:].indirect(offsets[:]))
        for q in range(SCALE_ROWS // 4):
            rows = slice(SCALE_AT + 4 * q, SCALE_AT + 4 * q + 4)
            nc.sync.dma_start(planes[32 * q : 32 * q + 4, :].bitcast(I32), picked_bytes[rows, :].bitcast(I32))

        nc.sync.dma_start(e_window[:, E_HEAD:], e_rows[:, E_HEAD:])

        y = {}
        for b in range(BLOCKS):
            y[b] = keep.tile([P, 2, S], F32, name=f"y_{b}")
            for part, table in ((RE, yr), (IM, yi)):
                nc.sync.dma_start(y[b][:, part, :], table[b * P : (b + 1) * P, :])

        def grouped_view(tile):
            return tile[:].rearrange("p (c i) j -> p c j i", i=LINE)

        def raw_view(tile):
            return tile[:].rearrange("p j (c i) -> p c j i", i=LINE)

        first_block, second_block = slice(0, P // LINE), slice(P // LINE, N // LINE)
        wi_bf = keep.tile([P, N, PACK], BF16, name="wi_bf", align_bytes=64)
        nc.scalar.copy(grouped_view(wi_bf), raw_view(wi_raw))
        wr_bf = keep.tile([P, N, PACK], BF16, name="wr_bf", align_bytes=64)
        nc.scalar.copy(grouped_view(wr_bf)[:, second_block], raw_view(wr_raw)[:, second_block])
        neg_bf = keep.tile([P, N, PACK], BF16, name="neg_bf", align_bytes=64)

        quant = {}

        def quantise(name, src):
            codes = keep.tile([P, N], U32, name=name + "_codes", align_bytes=64)
            scales = keep.tile([P, N], U8, name=name + "_scales", align_bytes=64)
            nc.vector.quantize_mx(
                out=codes[:].bitcast(FP8X4), scales=scales[:], in_=src[:].rearrange("p n j -> p (n j)")
            )
            quant[name] = (codes, scales)

        def pick_words(name, window):
            halves = []
            for h in range(HALVES):
                picked = keep.tile([P, HALF], U32, name=f"{name}_picked_{h}", align_bytes=64)
                cols = slice(h * HALF // 16, (h + 1) * HALF // 16)
                nc.vector.tensor_copy(picked[:], window[:].bitcast(U32).indirect(offsets[:, cols]))
                halves.append(picked)
            return halves

        nc.vector.tensor_scalar(neg_bf[:], wi_bf[:], -1.0, None, ALU.mult)
        quantise("wi", wi_bf)
        nc.vector.tensor_copy(grouped_view(wr_bf)[:, first_block], raw_view(wr_raw)[:, first_block])
        quantise("neg", neg_bf)
        quantise("wr", wr_bf)
        x_picked = pick_words("x", x_window)
        e_picked = pick_words("e", e_window)

        def entries(h, base=0):
            return slice(base + h * HALF, base + (h + 1) * HALF)

        def groups(h):
            return slice(h * HALF_GROUPS, (h + 1) * HALF_GROUPS)

        def product(dst, weight, b, words, plane, start, stop):
            codes, scales = quant[weight]
            cols = slice(b * P, (b + 1) * P)
            nc.tensor.matmul_mx(
                out=dst, lhsT=codes[:, cols].bitcast(FP8X4), lhsT_scale=scales[:, cols],
                rhs=words.bitcast(FP8X4), rhs_scale=plane, start=start, stop=stop,
            )

        acc = {
            (b, h): psum.tile([P, 2, HALF], F32, name=f"acc_{b}_{h}") for b in range(BLOCKS) for h in range(HALVES)
        }
        for h in range(HALVES):
            for b in range(BLOCKS):
                product(acc[b, h][:, IM, :], "wi", b, x_picked[h][:], planes[:, entries(h)], True, False)
                product(acc[b, h][:, RE, :], "wr", b, x_picked[h][:], planes[:, entries(h)], False, False)
        for h in range(HALVES):
            for b in range(BLOCKS):
                product(acc[b, h][:, RE, :], "neg", b, e_picked[h][:], planes[:, entries(h, S)], False, False)
                product(acc[b, h][:, IM, :], "wr", b, e_picked[h][:], planes[:, entries(h, S)], False, True)

        sq = [keep.tile([P, 2, D, GROUPS], F32, name=f"sq_{b}") for b in range(BLOCKS)]
        total = [keep.tile([P, GROUPS], F32, name=f"total_{b}") for b in range(BLOCKS)]
        magnitude = [keep.tile([P, GROUPS], F32, name=f"magnitude_{b}") for b in range(BLOCKS)]
        prod = [keep.tile([P, HALVES, 2, HALF], F32, name=f"prod_{b}") for b in range(BLOCKS)]

        def multiply(b, h):
            nc.vector.tensor_tensor(prod[b][:, h], acc[b, h][:], y[b][:, :, entries(h)], ALU.mult)

        def square(b, h, parts=slice(RE, IM + 1)):
            nc.scalar.activation(
                sq[b][:, parts, :, groups(h)], acc[b, h][:, parts, :].rearrange("p c (v d) -> p c d v", d=D),
                ACT.Square, scale=math.sqrt(0.6),
            )

        def sum_products(b, h):
            nc.vector.tensor_reduce(
                total[b][:, groups(h)], prod[b][:, h].rearrange("p c (v d) -> p v c d", d=D), AXIS.XY, ALU.add
            )

        def sum_products_shared(b):
            both = keep.tile([P, HALVES, HALF], F32, name=f"both_{b}")
            nc.gpsimd.tensor_tensor(both[:], prod[b][:, :, RE, :], prod[b][:, :, IM, :], ALU.add)
            nc.vector.tensor_reduce(total[b][:], both[:].rearrange("p h (v d) -> p (h v) d", d=D), AXIS.X, ALU.add)

        turned = [psum.tile([P, P], F32, name=f"turned_{b}") for b in range(BLOCKS)]
        power = [psum.tile([P, P], F32, name=f"power_{b}") for b in range(BLOCKS)]

        def sum_squares(b):
            for i in range(2 * D):
                nc.tensor.matmul(
                    turned[b][:], sq[b][:, i // D, i % D, :], identity[:],
                    start=(i == 0), stop=(i == 2 * D - 1), is_transpose=True,
                )

        def turn_back(b):
            turned_sb = keep.tile([P, P], F32, name=f"turned_sb_{b}")
            nc.scalar.copy(turned_sb[:], turned[b][:])
            nc.tensor.transpose(power[b][:], turned_sb[:], identity[:])

        def finish(b):
            result = keep.tile([P, GROUPS], F32, name=f"result_{b}")
            nc.vector.scalar_tensor_tensor(result[:], power[b][:], 0.12, magnitude[b][:], ALU.add, ALU.subtract)
            nc.sync.dma_start(out[b * P : (b + 1) * P, :], result[:])

        square(1, 0)
        square(1, 1)
        multiply(0, 0)
        multiply(0, 1)
        square(0, 0)
        square(0, 1, slice(RE, RE + 1))
        square(0, 1, slice(IM, IM + 1))
        sum_squares(1)
        sum_squares(0)
        turn_back(1)
        turn_back(0)
        multiply(1, 0)
        multiply(1, 1)
        sum_products(1, 0)
        sum_products_shared(0)
        sum_products(1, 1)
        nc.vector.scalar_tensor_tensor(magnitude[1][:], total[1][:], -1.0, total[1][:], ALU.mult, ALU.max)
        finish(1)
        nc.scalar.activation(magnitude[0][:], total[0][:], ACT.Abs)
        finish(0)
